import numpy as np
import ml_dtypes


def mxq(x, axis, fmt="e4m3"):
    dtype, down = {"e4m3": (ml_dtypes.float8_e4m3fn, 7), "e5m2": (ml_dtypes.float8_e5m2, 14)}[fmt]
    v = np.moveaxis(np.asarray(x, np.float32).astype(ml_dtypes.bfloat16).astype(np.float64), axis, -1)
    blocks = v.reshape(v.shape[:-1] + (-1, 32))
    amax = np.abs(blocks).max(-1, keepdims=True)
    byte = np.maximum(np.where(amax > 0, np.frexp(amax)[1] - 1 + 127, 0) - down, 1)
    scale = np.exp2(byte - 127.0)
    codes = (blocks / scale).astype(np.float32).astype(dtype).astype(np.float64)
    return np.moveaxis((codes * scale).reshape(v.shape), -1, axis)


WIDE = False


def mx_kscale(k):
    if not WIDE:
        return np.ones(k)
    levels = np.array([10, -10, 5, -5, 0])
    if k % 512:
        return np.exp2(np.random.permutation(np.resize(levels, k // 32))).repeat(32)
    a = np.empty((k // 512, 16))
    for p in range(k // 512):
        a[p, :8] = np.random.permutation(np.resize(levels, 8))
        for g in range(8):
            far = levels[np.abs(levels - a[p, g]) >= 10]
            a[p, g + 8] = far[np.random.randint(len(far))]
    return np.exp2(a.ravel()).repeat(32)


def f64(x):
    return np.asarray(x).astype(np.float64)


def striped(idx):
    return np.tile(idx.reshape(-1, 16).T, (8, 1)).astype(np.uint16)


def unstriped(offs):
    return offs[:16].T.reshape(-1).astype(np.int64)


E2M1 = np.array([0.0, 0.5, 1.0, 1.5, 2.0, 3.0, 4.0, 6.0, -0.0, -0.5, -1.0, -1.5, -2.0, -3.0, -4.0, -6.0])


def pack_fp4(w):
    k, n = w.shape
    w = f64(np.asarray(w, np.float32).astype(ml_dtypes.bfloat16)).reshape(k // 32, 32, n)
    amax = np.abs(w).max(1)
    mant, ex = np.frexp(amax / 6.0)
    byte = np.clip(np.where(amax > 0, np.where(mant > 0.5, ex, ex - 1) + 127, 1), 1, 254)
    scaled = (w * np.exp2(127.0 - byte)[:, None, :]).reshape(k, n).astype(np.float32)
    c = np.ascontiguousarray(scaled.reshape(k // 512, 128, 4, n).transpose(0, 1, 3, 2)).astype(ml_dtypes.float4_e2m1fn).view(np.uint8) & 0xF
    words = (c[..., 0::2] | (c[..., 1::2] << 4)).reshape(k // 512, 128, 2 * n)
    return np.ascontiguousarray(words), np.ascontiguousarray(byte.astype(np.uint8).reshape(k // 512, 16, n))


def unpack_fp4(words, scales):
    g, _, n = scales.shape
    words = np.ascontiguousarray(words).reshape(g, 128, n, 2)
    nib = np.empty((g, 128, n, 4), np.uint8)
    nib[..., 0::2] = words & 0xF
    nib[..., 1::2] = words >> 4
    vals = E2M1[nib] * np.repeat(np.exp2(scales.astype(np.float64) - 127.0), 8, axis=1)[..., None]
    return vals.transpose(0, 1, 3, 2).reshape(g * 512, n)


K, T, S, N, U = 512, 4096, 1024, 128, 2048


def setup_inputs():
    n = np.random.standard_normal
    s = mx_kscale(K)[:, None]
    packed_w1 = pack_fp4(n((K, N)) / np.sqrt(K) / s)
    return {
        "xT": (n((K, T)) * s).astype(np.float32),
        "mem": n((N, U)).astype(np.float32),
        "w1_words": packed_w1[0],
        "w1_scales": packed_w1[1],
        "offs": striped(np.random.permutation(T)[:S]),
        "slot": striped(np.random.permutation(U)[:S]),
    }


def reference(xT, mem, w1_words, w1_scales, offs, slot):
    xq = mxq(f64(xT)[:, unstriped(offs)], 0, "e4m3")
    y = np.tanh(unpack_fp4(w1_words, w1_scales).T @ xq)
    out = f64(mem).copy()
    out[:, unstriped(slot)] = y
    return out

@@ -1,0 +1,95 @@
+from contextlib import ExitStack
+
+import concourse.mybir as mybir
+
+K, T, S, N, U = 512, 4096, 1024, 128, 2048
+FLOPS = 2 * K * S * N
+
+F32 = mybir.dt.float32
+BF16 = mybir.dt.bfloat16
+I32 = mybir.dt.int32
+U32 = mybir.dt.uint32
+U16 = mybir.dt.uint16
+U8 = mybir.dt.uint8
+FP8X4 = mybir.dt.float8_e4m3fn_x4
+FP4X4 = mybir.dt.float4_e2m1fn_x4
+COPY = mybir.ActivationFunctionType.Copy
+TANH = mybir.ActivationFunctionType.Tanh
+
+P = 128
+PACK = 4
+HALF = S // 2
+STRIPE = 16
+PLANE_CHUNKS = ((4096,), (2048, 2048), (1024, 1024, 1024, 1024), (1024, 1024, 1024, 768, 256))
+PIECES = ((0, 256), (256, 256), (512, 512))
+SCATTERS = ((0, 256), (256, 768))
+
+
+def tile_picked_kvput_tanh_e_kernel(tc, xT, mem, w1_words, w1_scales, offs, slot, out):
+    nc = tc.nc
+    with ExitStack() as ctx:
+        keep = ctx.enter_context(tc.tile_pool(name="keep", bufs=1))
+        psum = ctx.enter_context(tc.psum_pool(name="psum", bufs=1))
+
+        offsets = keep.tile([P, S // STRIPE], U16, name="offsets")
+        slots = keep.tile([P, S // STRIPE], U16, name="slots")
+        planes = [keep.tile([P, T], F32, name="plane%d" % t, align_bytes=64) for t in range(PACK)]
+        rounded = {t: keep.tile([P, T], BF16, name="rounded%d" % t, align_bytes=64) for t in (2, 3)}
+        picked = [keep.tile([P, HALF, PACK], BF16, name="picked%d" % h, align_bytes=64) for h in range(2)]
+        w_words = keep.tile([P, 2 * N], U8, name="w_words", align_bytes=64)
+        w_scales = keep.tile([P, N], U8, name="w_scales", align_bytes=64)
+        store = keep.tile([P, U], F32, name="store", align_bytes=64)
+        y = keep.tile([P, S], F32, name="y", align_bytes=64)
+
+        nc.gpsimd.memset(w_scales[:], 0)
+        nc.gpsimd.dma_start(out=w_words[:].bitcast(I32), in_=w1_words[0].bitcast(I32))
+        for q in range(4):
+            nc.gpsimd.dma_start(out=w_scales[32 * q : 32 * q + 4, :].bitcast(I32), in_=w1_scales[0, 4 * q : 4 * q + 4, :].bitcast(I32))
+
+        rows = xT.rearrange("(p t) c -> p t c", t=PACK)
+        for t in range(PACK):
+            c0 = 0
+            for width in PLANE_CHUNKS[t]:
+                cols = slice(c0, c0 + width)
+                nc.sync.dma_start(out=planes[t][:, cols], in_=rows[:, t, cols])
+                if t == 3 and c0 < 2048:
+                    nc.vector.tensor_copy(rounded[t][:, cols], planes[t][:, cols])
+                elif t in rounded:
+                    nc.scalar.activation(rounded[t][:, cols], planes[t][:, cols], COPY)
+                c0 = c0 + width
+            if t == 0:
+                nc.sync.dma_start(offsets[:], offs)
+            if t == 1:
+                nc.sync.dma_start(slots[:], slot)
+            for h in range(2):
+                entries = offsets[:, h * HALF // STRIPE : (h + 1) * HALF // STRIPE]
+                if h == 1 and t in rounded:
+                    nc.scalar.activation(picked[h][:, :, t], rounded[t][:].indirect(entries), COPY)
+                else:
+                    nc.vector.tensor_copy(picked[h][:, :, t], planes[t][:].indirect(entries))
+        nc.sync.dma_start(out=store[:], in_=mem)
+
+        for i, (j0, n) in enumerate(PIECES):
+            codes = keep.tile([P, n], U32, name="codes%d" % i, align_bytes=64)
+            scales = keep.tile([P, n], U8, name="scales%d" % i, align_bytes=64)
+            h, a = divmod(j0, HALF)
+            nc.vector.quantize_mx(
+                out=codes[:].bitcast(FP8X4),
+                scales=scales[:],
+                in_=picked[h][:, a : a + n, :].rearrange("p n t -> p (n t)"),
+            )
+            acc = psum.tile([P, n], F32, name="acc%d" % i)
+            nc.tensor.matmul_mx(
+                out=acc[:],
+                lhsT=w_words[:].bitcast(FP4X4),
+                lhsT_scale=w_scales[:],
+                rhs=codes[:].bitcast(FP8X4),
+                rhs_scale=scales[:],
+                start=True,
+                stop=True,
+            )
+            nc.scalar.activation(y[:, j0 : j0 + n], acc[:], TANH)
+
+        for j0, n in SCATTERS:
+            nc.vector.tensor_copy(store[:].indirect(slots[:, j0 // STRIPE : (j0 + n) // STRIPE]), y[:, j0 : j0 + n])
+        nc.sync.dma_start(out=out, in_=store[:])

@@ -20,8 +20,9 @@ P = 128
 PACK = 4
 HALF = S // 2
 STRIPE = 16
-PLANE_CHUNKS = ((4096,), (2048, 2048), (1024, 1024, 1024, 1024), (1024, 1024, 1024, 768, 256))
-PIECES = ((0, 256), (256, 256), (512, 512))
+PLANE_ORDER = (2, 0, 1, 3)
+PLANE_CHUNKS = {2: (4096,), 0: (4096,), 1: (4096,), 3: (1024, 1024, 1024, 512, 256, 256)}
+PIECES = ((0, 128), (128, 128), (256, 256), (512, 512))
 SCATTERS = ((0, 256), (256, 768))
 
 
@@ -41,23 +42,23 @@ def tile_picked_kvput_tanh_e_kernel(tc, xT, mem, w1_words, w1_scales, offs, slot
         store = keep.tile([P, U], F32, name="store", align_bytes=64)
         y = keep.tile([P, S], F32, name="y", align_bytes=64)
 
-        nc.gpsimd.memset(w_scales[:], 0)
-        nc.gpsimd.dma_start(out=w_words[:].bitcast(I32), in_=w1_words[0].bitcast(I32))
+        nc.vector.memset(w_scales[:].bitcast(I32), 0)
+        nc.scalar.dma_start(out=w_words[:].bitcast(I32), in_=w1_words[0].bitcast(I32))
         for q in range(4):
-            nc.gpsimd.dma_start(out=w_scales[32 * q : 32 * q + 4, :].bitcast(I32), in_=w1_scales[0, 4 * q : 4 * q + 4, :].bitcast(I32))
+            nc.scalar.dma_start(out=w_scales[32 * q : 32 * q + 4, :].bitcast(I32), in_=w1_scales[0, 4 * q : 4 * q + 4, :].bitcast(I32))
 
         rows = xT.rearrange("(p t) c -> p t c", t=PACK)
-        for t in range(PACK):
+        for t in PLANE_ORDER:
             c0 = 0
             for width in PLANE_CHUNKS[t]:
                 cols = slice(c0, c0 + width)
                 nc.sync.dma_start(out=planes[t][:, cols], in_=rows[:, t, cols])
-                if t == 3 and c0 < 2048:
+                if t == 3 and c0 >= 3072:
                     nc.vector.tensor_copy(rounded[t][:, cols], planes[t][:, cols])
                 elif t in rounded:
                     nc.scalar.activation(rounded[t][:, cols], planes[t][:, cols], COPY)
                 c0 = c0 + width
-            if t == 0:
+            if t == 2:
                 nc.sync.dma_start(offsets[:], offs)
             if t == 1:
                 nc.sync.dma_start(slots[:], slot)

@@ -21,7 +21,7 @@ PACK = 4
 HALF = S // 2
 STRIPE = 16
 PLANE_ORDER = (2, 0, 1, 3)
-PLANE_CHUNKS = {2: (4096,), 0: (4096,), 1: (4096,), 3: (1024, 1024, 1024, 512, 256, 256)}
+PLANE_CHUNKS = {2: (4096,), 0: (4096,), 1: (4096,), 3: (1024, 1024, 768, 768, 256, 256)}
 PIECES = ((0, 128), (128, 128), (256, 256), (512, 512))
 SCATTERS = ((0, 256), (256, 768))
 
@@ -43,9 +43,6 @@ def tile_picked_kvput_tanh_e_kernel(tc, xT, mem, w1_words, w1_scales, offs, slot
         y = keep.tile([P, S], F32, name="y", align_bytes=64)
 
         nc.vector.memset(w_scales[:].bitcast(I32), 0)
-        nc.scalar.dma_start(out=w_words[:].bitcast(I32), in_=w1_words[0].bitcast(I32))
-        for q in range(4):
-            nc.scalar.dma_start(out=w_scales[32 * q : 32 * q + 4, :].bitcast(I32), in_=w1_scales[0, 4 * q : 4 * q + 4, :].bitcast(I32))
 
         rows = xT.rearrange("(p t) c -> p t c", t=PACK)
         for t in PLANE_ORDER:
@@ -53,22 +50,25 @@ def tile_picked_kvput_tanh_e_kernel(tc, xT, mem, w1_words, w1_scales, offs, slot
             for width in PLANE_CHUNKS[t]:
                 cols = slice(c0, c0 + width)
                 nc.sync.dma_start(out=planes[t][:, cols], in_=rows[:, t, cols])
-                if t == 3 and c0 >= 3072:
+                if t == 3 and c0 == 2816:
                     nc.vector.tensor_copy(rounded[t][:, cols], planes[t][:, cols])
                 elif t in rounded:
                     nc.scalar.activation(rounded[t][:, cols], planes[t][:, cols], COPY)
                 c0 = c0 + width
             if t == 2:
                 nc.sync.dma_start(offsets[:], offs)
-            if t == 1:
-                nc.sync.dma_start(slots[:], slot)
             for h in range(2):
                 entries = offsets[:, h * HALF // STRIPE : (h + 1) * HALF // STRIPE]
                 if h == 1 and t in rounded:
                     nc.scalar.activation(picked[h][:, :, t], rounded[t][:].indirect(entries), COPY)
                 else:
                     nc.vector.tensor_copy(picked[h][:, :, t], planes[t][:].indirect(entries))
-        nc.sync.dma_start(out=store[:], in_=mem)
+        nc.sync.dma_start(out=store[:, : U // 2], in_=mem[:, : U // 2])
+        nc.sync.dma_start(out=w_words[:].bitcast(I32), in_=w1_words[0].bitcast(I32))
+        for q in range(4):
+            nc.sync.dma_start(out=w_scales[32 * q : 32 * q + 4, :].bitcast(I32), in_=w1_scales[0, 4 * q : 4 * q + 4, :].bitcast(I32))
+        nc.sync.dma_start(out=store[:, U // 2 :], in_=mem[:, U // 2 :])
+        nc.sync.dma_start(slots[:], slot)
 
         for i, (j0, n) in enumerate(PIECES):
             codes = keep.tile([P, n], U32, name="codes%d" % i, align_bytes=64)

from contextlib import ExitStack

import concourse.mybir as mybir

K, T, S, N, U = 512, 4096, 1024, 128, 2048
FLOPS = 2 * K * S * N

F32 = mybir.dt.float32
BF16 = mybir.dt.bfloat16
I32 = mybir.dt.int32
U32 = mybir.dt.uint32
U16 = mybir.dt.uint16
U8 = mybir.dt.uint8
FP8X4 = mybir.dt.float8_e4m3fn_x4
FP4X4 = mybir.dt.float4_e2m1fn_x4
COPY = mybir.ActivationFunctionType.Copy
TANH = mybir.ActivationFunctionType.Tanh

P = 128
PACK = 4
HALF = S // 2
STRIPE = 16
PLANE_ORDER = (2, 0, 1, 3)
PLANE_CHUNKS = {2: (4096,), 0: (4096,), 1: (4096,), 3: (1024, 1024, 768, 768, 256, 256)}
PIECES = ((0, 128), (128, 128), (256, 256), (512, 512))
SCATTERS = ((0, 256), (256, 768))


def tile_picked_kvput_tanh_e_kernel(tc, xT, mem, w1_words, w1_scales, offs, slot, out):
    nc = tc.nc
    with ExitStack() as ctx:
        keep = ctx.enter_context(tc.tile_pool(name="keep", bufs=1))
        psum = ctx.enter_context(tc.psum_pool(name="psum", bufs=1))

        offsets = keep.tile([P, S // STRIPE], U16, name="offsets")
        slots = keep.tile([P, S // STRIPE], U16, name="slots")
        planes = [keep.tile([P, T], F32, name="plane%d" % t, align_bytes=64) for t in range(PACK)]
        rounded = {t: keep.tile([P, T], BF16, name="rounded%d" % t, align_bytes=64) for t in (2, 3)}
        picked = [keep.tile([P, HALF, PACK], BF16, name="picked%d" % h, align_bytes=64) for h in range(2)]
        w_words = keep.tile([P, 2 * N], U8, name="w_words", align_bytes=64)
        w_scales = keep.tile([P, N], U8, name="w_scales", align_bytes=64)
        store = keep.tile([P, U], F32, name="store", align_bytes=64)
        y = keep.tile([P, S], F32, name="y", align_bytes=64)

        nc.vector.memset(w_scales[:].bitcast(I32), 0)

        rows = xT.rearrange("(p t) c -> p t c", t=PACK)
        for t in PLANE_ORDER:
            c0 = 0
            for width in PLANE_CHUNKS[t]:
                cols = slice(c0, c0 + width)
                nc.sync.dma_start(out=planes[t][:, cols], in_=rows[:, t, cols])
                if t == 3 and c0 == 2816:
                    nc.vector.tensor_copy(rounded[t][:, cols], planes[t][:, cols])
                elif t in rounded:
                    nc.scalar.activation(rounded[t][:, cols], planes[t][:, cols], COPY)
                c0 = c0 + width
            if t == 2:
                nc.sync.dma_start(offsets[:], offs)
            for h in range(2):
                entries = offsets[:, h * HALF // STRIPE : (h + 1) * HALF // STRIPE]
                if h == 1 and t in rounded:
                    nc.scalar.activation(picked[h][:, :, t], rounded[t][:].indirect(entries), COPY)
                else:
                    nc.vector.tensor_copy(picked[h][:, :, t], planes[t][:].indirect(entries))
        nc.sync.dma_start(out=store[:, : U // 2], in_=mem[:, : U // 2])
        nc.sync.dma_start(out=w_words[:].bitcast(I32), in_=w1_words[0].bitcast(I32))
        for q in range(4):
            nc.sync.dma_start(out=w_scales[32 * q : 32 * q + 4, :].bitcast(I32), in_=w1_scales[0, 4 * q : 4 * q + 4, :].bitcast(I32))
        nc.sync.dma_start(out=store[:, U // 2 :], in_=mem[:, U // 2 :])
        nc.sync.dma_start(slots[:], slot)

        for i, (j0, n) in enumerate(PIECES):
            codes = keep.tile([P, n], U32, name="codes%d" % i, align_bytes=64)
            scales = keep.tile([P, n], U8, name="scales%d" % i, align_bytes=64)
            h, a = divmod(j0, HALF)
            nc.vector.quantize_mx(
                out=codes[:].bitcast(FP8X4),
                scales=scales[:],
                in_=picked[h][:, a : a + n, :].rearrange("p n t -> p (n t)"),
            )
            acc = psum.tile([P, n], F32, name="acc%d" % i)
            nc.tensor.matmul_mx(
                out=acc[:],
                lhsT=w_words[:].bitcast(FP4X4),
                lhsT_scale=w_scales[:],
                rhs=codes[:].bitcast(FP8X4),
                rhs_scale=scales[:],
                start=True,
                stop=True,
            )
            nc.scalar.activation(y[:, j0 : j0 + n], acc[:], TANH)

        for j0, n in SCATTERS:
            nc.vector.tensor_copy(store[:].indirect(slots[:, j0 // STRIPE : (j0 + n) // STRIPE]), y[:, j0 : j0 + n])
        nc.sync.dma_start(out=out, in_=store[:])
